import numpy as np
import ml_dtypes

BF16 = ml_dtypes.bfloat16


def bf(x):
    return np.asarray(x, np.float32).astype(BF16)


def f32(x):
    return np.asarray(x, np.float32)


def f64(x):
    return np.asarray(x).astype(np.float64)


def striped(idx):
    return np.tile(idx.reshape(-1, 16).T, (8, 1))


S, K, M, N, B, Q = 512, 128, 256, 128, 2, 64


def setup_inputs():
    return {"base": bf(np.random.standard_normal((B, M, S))), "x": bf(np.random.standard_normal((K, N))), "w": bf(np.random.standard_normal((K, M)) / np.sqrt(K)), "offs": striped(np.random.permutation(S)[:N])}


def reference(base, x, w, offs):
    idx = offs[:16].T.reshape(-1)
    z = f64(base).copy()
    for i in range(B):
        z[i][:, idx[i * Q : (i + 1) * Q]] += f64(w).T @ f64(x)[:, i * Q : (i + 1) * Q]
    return z

@@ -1,0 +1,61 @@
+import concourse.mybir as mybir
+from concourse.masks import make_identity
+
+BF16, F32, U16 = mybir.dt.bfloat16, mybir.dt.float32, mybir.dt.uint16
+
+P = 128
+SEQS, FEATURES, TOKENS = 2, 256, 512
+CONTRACT, ENTRIES = 128, 128
+PIECE = ENTRIES // SEQS
+PIECE_COLS = PIECE // 16
+BLOCKS = FEATURES // P
+
+FLOPS = 2 * CONTRACT * FEATURES * ENTRIES
+
+
+def tile_scatter_matmul_kernel(tc, base, x, w, offs, out):
+    nc = tc.nc
+    pairs = [(i, a) for i in range(SEQS) for a in range(BLOCKS)]
+    with (
+        tc.tile_pool(name="held", bufs=1) as held,
+        tc.psum_pool(name="banks", bufs=1) as banks,
+    ):
+        offsets = held.tile([P, ENTRIES // 16], U16, name="offsets")
+        nc.sync.dma_start(offsets[:], offs)
+
+        base_tiles = {}
+        for n, (i, a) in enumerate(pairs):
+            base_tiles[(i, a)] = held.tile([P, TOKENS], BF16, name=f"base_{i}_{a}")
+            queue = nc.sync if n % 2 == 0 else nc.scalar
+            queue.dma_start(base_tiles[(i, a)][:], base[i, a * P : (a + 1) * P, :])
+        w_tile = held.tile([CONTRACT, FEATURES], BF16, name="w_tile")
+        nc.sync.dma_start(w_tile[:], w)
+        x_tile = held.tile([CONTRACT, ENTRIES], BF16, name="x_tile")
+        nc.scalar.dma_start(x_tile[:], x)
+
+        identity = held.tile([P, P], BF16, name="identity")
+        make_identity(nc, identity[:])
+
+        windows = {}
+        for i, a in pairs:
+            windows[(i, a)] = banks.tile([P, TOKENS], F32, name=f"window_{i}_{a}")
+            nc.tensor.matmul(windows[(i, a)][:], identity[:], base_tiles[(i, a)][:], start=True, stop=False)
+
+        for i, a in pairs:
+            piece = offsets[:, i * PIECE_COLS : (i + 1) * PIECE_COLS]
+            nc.tensor.matmul(
+                windows[(i, a)][:].indirect(piece),
+                w_tile[:, a * P : (a + 1) * P],
+                x_tile[:, i * PIECE : (i + 1) * PIECE],
+                start=False,
+                stop=True,
+            )
+
+        for n, (i, a) in enumerate(pairs):
+            staged = held.tile([P, TOKENS], F32, name=f"staged_{i}_{a}")
+            if n % 2 == 0:
+                nc.vector.tensor_copy(staged[:], windows[(i, a)][:])
+                nc.sync.dma_start(out[i, a * P : (a + 1) * P, :], staged[:])
+            else:
+                nc.scalar.copy(staged[:], windows[(i, a)][:])
+                nc.scalar.dma_start(out[i, a * P : (a + 1) * P, :], staged[:])

@@ -10,6 +10,8 @@ PIECE = ENTRIES // SEQS
 PIECE_COLS = PIECE // 16
 BLOCKS = FEATURES // P
 
+WARMUPS = 3
+
 FLOPS = 2 * CONTRACT * FEATURES * ENTRIES
 
 
@@ -20,14 +22,13 @@ def tile_scatter_matmul_kernel(tc, base, x, w, offs, out):
         tc.tile_pool(name="held", bufs=1) as held,
         tc.psum_pool(name="banks", bufs=1) as banks,
     ):
-        offsets = held.tile([P, ENTRIES // 16], U16, name="offsets")
-        nc.sync.dma_start(offsets[:], offs)
-
         base_tiles = {}
         for n, (i, a) in enumerate(pairs):
             base_tiles[(i, a)] = held.tile([P, TOKENS], BF16, name=f"base_{i}_{a}")
             queue = nc.sync if n % 2 == 0 else nc.scalar
             queue.dma_start(base_tiles[(i, a)][:], base[i, a * P : (a + 1) * P, :])
+        offsets = held.tile([P, ENTRIES // 16], U16, name="offsets")
+        nc.sync.dma_start(offsets[:], offs)
         w_tile = held.tile([CONTRACT, FEATURES], BF16, name="w_tile")
         nc.sync.dma_start(w_tile[:], w)
         x_tile = held.tile([CONTRACT, ENTRIES], BF16, name="x_tile")
@@ -35,6 +36,12 @@ def tile_scatter_matmul_kernel(tc, base, x, w, offs, out):
 
         identity = held.tile([P, P], BF16, name="identity")
         make_identity(nc, identity[:])
+
+        zeros = held.tile([P, TOKENS], BF16, name="zeros")
+        nc.vector.memset(zeros[:], 0.0)
+        unread = banks.tile([P, TOKENS], F32, name="unread")
+        for n in range(WARMUPS):
+            nc.tensor.matmul(unread[:], zeros[:, 0:P], zeros[:], start=True, stop=True)
 
         windows = {}
         for i, a in pairs:

@@ -8,6 +8,7 @@ SEQS, FEATURES, TOKENS = 2, 256, 512
 CONTRACT, ENTRIES = 128, 128
 PIECE = ENTRIES // SEQS
 PIECE_COLS = PIECE // 16
+HALF = TOKENS // 2
 BLOCKS = FEATURES // P
 
 WARMUPS = 3
@@ -60,9 +61,11 @@ def tile_scatter_matmul_kernel(tc, base, x, w, offs, out):
 
         for n, (i, a) in enumerate(pairs):
             staged = held.tile([P, TOKENS], F32, name=f"staged_{i}_{a}")
-            if n % 2 == 0:
-                nc.vector.tensor_copy(staged[:], windows[(i, a)][:])
-                nc.sync.dma_start(out[i, a * P : (a + 1) * P, :], staged[:])
-            else:
-                nc.scalar.copy(staged[:], windows[(i, a)][:])
-                nc.scalar.dma_start(out[i, a * P : (a + 1) * P, :], staged[:])
+            for h in range(2):
+                cols = slice(h * HALF, (h + 1) * HALF)
+                if n % 2 == 0:
+                    nc.vector.tensor_copy(staged[:, cols], windows[(i, a)][:, cols])
+                    nc.sync.dma_start(out[i, a * P : (a + 1) * P, cols], staged[:, cols])
+                else:
+                    nc.scalar.copy(staged[:, cols], windows[(i, a)][:, cols])
+                    nc.scalar.dma_start(out[i, a * P : (a + 1) * P, cols], staged[:, cols])

@@ -11,7 +11,10 @@ PIECE_COLS = PIECE // 16
 HALF = TOKENS // 2
 BLOCKS = FEATURES // P
 
-WARMUPS = 3
+WARMUPS = 2
+
+BETWEEN_RUNS = 24
+FILL_COLS = TOKENS * (SEQS * BLOCKS - 1) // BETWEEN_RUNS
 
 FLOPS = 2 * CONTRACT * FEATURES * ENTRIES
 
@@ -23,17 +26,17 @@ def tile_scatter_matmul_kernel(tc, base, x, w, offs, out):
         tc.tile_pool(name="held", bufs=1) as held,
         tc.psum_pool(name="banks", bufs=1) as banks,
     ):
+        offsets = held.tile([P, ENTRIES // 16], U16, name="offsets")
+        nc.sync.dma_start(offsets[:], offs)
+        w_tile = held.tile([CONTRACT, FEATURES], BF16, name="w_tile")
+        nc.scalar.dma_start(w_tile[:], w)
+        x_tile = held.tile([CONTRACT, ENTRIES], BF16, name="x_tile")
+        nc.scalar.dma_start(x_tile[:], x)
         base_tiles = {}
         for n, (i, a) in enumerate(pairs):
             base_tiles[(i, a)] = held.tile([P, TOKENS], BF16, name=f"base_{i}_{a}")
             queue = nc.sync if n % 2 == 0 else nc.scalar
             queue.dma_start(base_tiles[(i, a)][:], base[i, a * P : (a + 1) * P, :])
-        offsets = held.tile([P, ENTRIES // 16], U16, name="offsets")
-        nc.sync.dma_start(offsets[:], offs)
-        w_tile = held.tile([CONTRACT, FEATURES], BF16, name="w_tile")
-        nc.sync.dma_start(w_tile[:], w)
-        x_tile = held.tile([CONTRACT, ENTRIES], BF16, name="x_tile")
-        nc.scalar.dma_start(x_tile[:], x)
 
         identity = held.tile([P, P], BF16, name="identity")
         make_identity(nc, identity[:])
@@ -47,17 +50,33 @@ def tile_scatter_matmul_kernel(tc, base, x, w, offs, out):
         windows = {}
         for i, a in pairs:
             windows[(i, a)] = banks.tile([P, TOKENS], F32, name=f"window_{i}_{a}")
-            nc.tensor.matmul(windows[(i, a)][:], identity[:], base_tiles[(i, a)][:], start=True, stop=False)
 
-        for i, a in pairs:
-            piece = offsets[:, i * PIECE_COLS : (i + 1) * PIECE_COLS]
+        def fill(pair, width):
+            for c in range(0, TOKENS, width):
+                nc.tensor.matmul(
+                    windows[pair][:, c : c + width],
+                    identity[:],
+                    base_tiles[pair][:, c : c + width],
+                    start=(c == 0),
+                    stop=False,
+                )
+
+        def scatter(pair):
+            i, a = pair
             nc.tensor.matmul(
-                windows[(i, a)][:].indirect(piece),
+                windows[pair][:].indirect(offsets[:, i * PIECE_COLS : (i + 1) * PIECE_COLS]),
                 w_tile[:, a * P : (a + 1) * P],
                 x_tile[:, i * PIECE : (i + 1) * PIECE],
                 start=False,
                 stop=True,
             )
+
+        fill(pairs[0], TOKENS)
+        scatter(pairs[0])
+        for pair in pairs[1:]:
+            fill(pair, FILL_COLS)
+        for pair in pairs[1:]:
+            scatter(pair)
 
         for n, (i, a) in enumerate(pairs):
             staged = held.tile([P, TOKENS], F32, name=f"staged_{i}_{a}")

@@ -26,17 +26,18 @@ def tile_scatter_matmul_kernel(tc, base, x, w, offs, out):
         tc.tile_pool(name="held", bufs=1) as held,
         tc.psum_pool(name="banks", bufs=1) as banks,
     ):
-        offsets = held.tile([P, ENTRIES // 16], U16, name="offsets")
-        nc.sync.dma_start(offsets[:], offs)
-        w_tile = held.tile([CONTRACT, FEATURES], BF16, name="w_tile")
-        nc.scalar.dma_start(w_tile[:], w)
-        x_tile = held.tile([CONTRACT, ENTRIES], BF16, name="x_tile")
-        nc.scalar.dma_start(x_tile[:], x)
         base_tiles = {}
-        for n, (i, a) in enumerate(pairs):
+        for i, a in pairs:
             base_tiles[(i, a)] = held.tile([P, TOKENS], BF16, name=f"base_{i}_{a}")
-            queue = nc.sync if n % 2 == 0 else nc.scalar
-            queue.dma_start(base_tiles[(i, a)][:], base[i, a * P : (a + 1) * P, :])
+        offsets = held.tile([P, ENTRIES // 16], U16, name="offsets")
+        x_tile = held.tile([CONTRACT, ENTRIES], BF16, name="x_tile")
+        w_tile = held.tile([CONTRACT, FEATURES], BF16, name="w_tile")
+        for n, (i, a) in enumerate(pairs):
+            nc.sync.dma_start(base_tiles[(i, a)][:], base[i, a * P : (a + 1) * P, :])
+            if n == 0:
+                nc.sync.dma_start(offsets[:], offs)
+                nc.sync.dma_start(x_tile[:], x)
+                nc.sync.dma_start(w_tile[:], w)
 
         identity = held.tile([P, P], BF16, name="identity")
         make_identity(nc, identity[:])

@@ -14,7 +14,9 @@ BLOCKS = FEATURES // P
 WARMUPS = 2
 
 BETWEEN_RUNS = 24
-FILL_COLS = TOKENS * (SEQS * BLOCKS - 1) // BETWEEN_RUNS
+FILL_PIECES = BETWEEN_RUNS // BLOCKS
+FILL_COLS = 44
+assert (FILL_PIECES - 1) * FILL_COLS < TOKENS <= FILL_PIECES * FILL_COLS
 
 FLOPS = 2 * CONTRACT * FEATURES * ENTRIES
 
@@ -32,9 +34,10 @@ def tile_scatter_matmul_kernel(tc, base, x, w, offs, out):
         offsets = held.tile([P, ENTRIES // 16], U16, name="offsets")
         x_tile = held.tile([CONTRACT, ENTRIES], BF16, name="x_tile")
         w_tile = held.tile([CONTRACT, FEATURES], BF16, name="w_tile")
-        for n, (i, a) in enumerate(pairs):
-            nc.sync.dma_start(base_tiles[(i, a)][:], base[i, a * P : (a + 1) * P, :])
-            if n == 0:
+        for i in range(SEQS):
+            for a in range(BLOCKS):
+                nc.sync.dma_start(base_tiles[(i, a)][:], base[i, a * P : (a + 1) * P, :])
+            if i == 0:
                 nc.sync.dma_start(offsets[:], offs)
                 nc.sync.dma_start(x_tile[:], x)
                 nc.sync.dma_start(w_tile[:], w)
@@ -54,12 +57,9 @@ def tile_scatter_matmul_kernel(tc, base, x, w, offs, out):
 
         def fill(pair, width):
             for c in range(0, TOKENS, width):
+                cols = slice(c, min(c + width, TOKENS))
                 nc.tensor.matmul(
-                    windows[pair][:, c : c + width],
-                    identity[:],
-                    base_tiles[pair][:, c : c + width],
-                    start=(c == 0),
-                    stop=False,
+                    windows[pair][:, cols], identity[:], base_tiles[pair][:, cols], start=(c == 0), stop=False
                 )
 
         def scatter(pair):
@@ -72,12 +72,11 @@ def tile_scatter_matmul_kernel(tc, base, x, w, offs, out):
                 stop=True,
             )
 
-        fill(pairs[0], TOKENS)
-        scatter(pairs[0])
-        for pair in pairs[1:]:
-            fill(pair, FILL_COLS)
-        for pair in pairs[1:]:
-            scatter(pair)
+        for i in range(SEQS):
+            for a in range(BLOCKS):
+                fill((i, a), TOKENS if i == 0 else FILL_COLS)
+            for a in range(BLOCKS):
+                scatter((i, a))
 
         for n, (i, a) in enumerate(pairs):
             staged = held.tile([P, TOKENS], F32, name=f"staged_{i}_{a}")

@@ -11,7 +11,7 @@ PIECE_COLS = PIECE // 16
 HALF = TOKENS // 2
 BLOCKS = FEATURES // P
 
-WARMUPS = 2
+WARMUPS = 13
 
 BETWEEN_RUNS = 24
 FILL_PIECES = BETWEEN_RUNS // BLOCKS
@@ -42,14 +42,14 @@ def tile_scatter_matmul_kernel(tc, base, x, w, offs, out):
                 nc.sync.dma_start(x_tile[:], x)
                 nc.sync.dma_start(w_tile[:], w)
 
+        zeros = held.tile([P, P], BF16, name="zeros")
+        nc.gpsimd.memset(zeros[:], 0.0)
+        unread = banks.tile([P, P], F32, name="unread")
+        for n in range(WARMUPS):
+            nc.tensor.matmul(unread[:], zeros[:], zeros[:], start=True, stop=True)
+
         identity = held.tile([P, P], BF16, name="identity")
         make_identity(nc, identity[:])
-
-        zeros = held.tile([P, TOKENS], BF16, name="zeros")
-        nc.vector.memset(zeros[:], 0.0)
-        unread = banks.tile([P, TOKENS], F32, name="unread")
-        for n in range(WARMUPS):
-            nc.tensor.matmul(unread[:], zeros[:, 0:P], zeros[:], start=True, stop=True)
 
         windows = {}
         for i, a in pairs:

@@ -11,7 +11,7 @@ PIECE_COLS = PIECE // 16
 HALF = TOKENS // 2
 BLOCKS = FEATURES // P
 
-WARMUPS = 13
+WARMUPS = 9
 
 BETWEEN_RUNS = 24
 FILL_PIECES = BETWEEN_RUNS // BLOCKS

@@ -9,6 +9,7 @@ CONTRACT, ENTRIES = 128, 128
 PIECE = ENTRIES // SEQS
 PIECE_COLS = PIECE // 16
 HALF = TOKENS // 2
+QUARTER = TOKENS // 4
 BLOCKS = FEATURES // P
 
 WARMUPS = 9
@@ -80,8 +81,8 @@ def tile_scatter_matmul_kernel(tc, base, x, w, offs, out):
 
         for n, (i, a) in enumerate(pairs):
             staged = held.tile([P, TOKENS], F32, name=f"staged_{i}_{a}")
-            for h in range(2):
-                cols = slice(h * HALF, (h + 1) * HALF)
+            cut = QUARTER if n == 0 else HALF
+            for cols in (slice(0, cut), slice(cut, TOKENS)):
                 if n % 2 == 0:
                     nc.vector.tensor_copy(staged[:, cols], windows[(i, a)][:, cols])
                     nc.sync.dma_start(out[i, a * P : (a + 1) * P, cols], staged[:, cols])

@@ -8,7 +8,6 @@ SEQS, FEATURES, TOKENS = 2, 256, 512
 CONTRACT, ENTRIES = 128, 128
 PIECE = ENTRIES // SEQS
 PIECE_COLS = PIECE // 16
-HALF = TOKENS // 2
 QUARTER = TOKENS // 4
 BLOCKS = FEATURES // P
 
@@ -81,8 +80,7 @@ def tile_scatter_matmul_kernel(tc, base, x, w, offs, out):
 
         for n, (i, a) in enumerate(pairs):
             staged = held.tile([P, TOKENS], F32, name=f"staged_{i}_{a}")
-            cut = QUARTER if n == 0 else HALF
-            for cols in (slice(0, cut), slice(cut, TOKENS)):
+            for cols in (slice(0, QUARTER), slice(QUARTER, TOKENS)):
                 if n % 2 == 0:
                     nc.vector.tensor_copy(staged[:, cols], windows[(i, a)][:, cols])
                     nc.sync.dma_start(out[i, a * P : (a + 1) * P, cols], staged[:, cols])

@@ -33,14 +33,15 @@ def tile_scatter_matmul_kernel(tc, base, x, w, offs, out):
             base_tiles[(i, a)] = held.tile([P, TOKENS], BF16, name=f"base_{i}_{a}")
         offsets = held.tile([P, ENTRIES // 16], U16, name="offsets")
         x_tile = held.tile([CONTRACT, ENTRIES], BF16, name="x_tile")
-        w_tile = held.tile([CONTRACT, FEATURES], BF16, name="w_tile")
+        w_blocks = [held.tile([CONTRACT, P], BF16, name=f"w_block_{a}") for a in range(BLOCKS)]
         for i in range(SEQS):
             for a in range(BLOCKS):
                 nc.sync.dma_start(base_tiles[(i, a)][:], base[i, a * P : (a + 1) * P, :])
             if i == 0:
                 nc.sync.dma_start(offsets[:], offs)
                 nc.sync.dma_start(x_tile[:], x)
-                nc.sync.dma_start(w_tile[:], w)
+                for b in range(BLOCKS):
+                    nc.sync.dma_start(w_blocks[b][:], w[:, b * P : (b + 1) * P])
 
         zeros = held.tile([P, P], BF16, name="zeros")
         nc.gpsimd.memset(zeros[:], 0.0)
@@ -66,7 +67,7 @@ def tile_scatter_matmul_kernel(tc, base, x, w, offs, out):
             i, a = pair
             nc.tensor.matmul(
                 windows[pair][:].indirect(offsets[:, i * PIECE_COLS : (i + 1) * PIECE_COLS]),
-                w_tile[:, a * P : (a + 1) * P],
+                w_blocks[a][:],
                 x_tile[:, i * PIECE : (i + 1) * PIECE],
                 start=False,
                 stop=True,

@@ -79,9 +79,16 @@ def tile_scatter_matmul_kernel(tc, base, x, w, offs, out):
             for a in range(BLOCKS):
                 scatter((i, a))
 
+        parts_of = {
+            (0, 0): (QUARTER, TOKENS),
+            (0, 1): (QUARTER, TOKENS),
+            (1, 0): (TOKENS // 2, TOKENS),
+            (1, 1): (TOKENS,),
+        }
         for n, (i, a) in enumerate(pairs):
             staged = held.tile([P, TOKENS], F32, name=f"staged_{i}_{a}")
-            for cols in (slice(0, QUARTER), slice(QUARTER, TOKENS)):
+            ends = parts_of[(i, a)]
+            for cols in [slice(c0, c1) for c0, c1 in zip((0,) + ends, ends)]:
                 if n % 2 == 0:
                     nc.vector.tensor_copy(staged[:, cols], windows[(i, a)][:, cols])
                     nc.sync.dma_start(out[i, a * P : (a + 1) * P, cols], staged[:, cols])

import concourse.mybir as mybir
from concourse.masks import make_identity

BF16, F32, U16 = mybir.dt.bfloat16, mybir.dt.float32, mybir.dt.uint16

P = 128
SEQS, FEATURES, TOKENS = 2, 256, 512
CONTRACT, ENTRIES = 128, 128
PIECE = ENTRIES // SEQS
PIECE_COLS = PIECE // 16
QUARTER = TOKENS // 4
BLOCKS = FEATURES // P

WARMUPS = 9

BETWEEN_RUNS = 24
FILL_PIECES = BETWEEN_RUNS // BLOCKS
FILL_COLS = 44
assert (FILL_PIECES - 1) * FILL_COLS < TOKENS <= FILL_PIECES * FILL_COLS

FLOPS = 2 * CONTRACT * FEATURES * ENTRIES


def tile_scatter_matmul_kernel(tc, base, x, w, offs, out):
    nc = tc.nc
    pairs = [(i, a) for i in range(SEQS) for a in range(BLOCKS)]
    with (
        tc.tile_pool(name="held", bufs=1) as held,
        tc.psum_pool(name="banks", bufs=1) as banks,
    ):
        base_tiles = {}
        for i, a in pairs:
            base_tiles[(i, a)] = held.tile([P, TOKENS], BF16, name=f"base_{i}_{a}")
        offsets = held.tile([P, ENTRIES // 16], U16, name="offsets")
        x_tile = held.tile([CONTRACT, ENTRIES], BF16, name="x_tile")
        w_blocks = [held.tile([CONTRACT, P], BF16, name=f"w_block_{a}") for a in range(BLOCKS)]
        for i in range(SEQS):
            for a in range(BLOCKS):
                nc.sync.dma_start(base_tiles[(i, a)][:], base[i, a * P : (a + 1) * P, :])
            if i == 0:
                nc.sync.dma_start(offsets[:], offs)
                nc.sync.dma_start(x_tile[:], x)
                for b in range(BLOCKS):
                    nc.sync.dma_start(w_blocks[b][:], w[:, b * P : (b + 1) * P])

        zeros = held.tile([P, P], BF16, name="zeros")
        nc.gpsimd.memset(zeros[:], 0.0)
        unread = banks.tile([P, P], F32, name="unread")
        for n in range(WARMUPS):
            nc.tensor.matmul(unread[:], zeros[:], zeros[:], start=True, stop=True)

        identity = held.tile([P, P], BF16, name="identity")
        make_identity(nc, identity[:])

        windows = {}
        for i, a in pairs:
            windows[(i, a)] = banks.tile([P, TOKENS], F32, name=f"window_{i}_{a}")

        def fill(pair, width):
            for c in range(0, TOKENS, width):
                cols = slice(c, min(c + width, TOKENS))
                nc.tensor.matmul(
                    windows[pair][:, cols], identity[:], base_tiles[pair][:, cols], start=(c == 0), stop=False
                )

        def scatter(pair):
            i, a = pair
            nc.tensor.matmul(
                windows[pair][:].indirect(offsets[:, i * PIECE_COLS : (i + 1) * PIECE_COLS]),
                w_blocks[a][:],
                x_tile[:, i * PIECE : (i + 1) * PIECE],
                start=False,
                stop=True,
            )

        for i in range(SEQS):
            for a in range(BLOCKS):
                fill((i, a), TOKENS if i == 0 else FILL_COLS)
            for a in range(BLOCKS):
                scatter((i, a))

        parts_of = {
            (0, 0): (QUARTER, TOKENS),
            (0, 1): (QUARTER, TOKENS),
            (1, 0): (TOKENS // 2, TOKENS),
            (1, 1): (TOKENS,),
        }
        for n, (i, a) in enumerate(pairs):
            staged = held.tile([P, TOKENS], F32, name=f"staged_{i}_{a}")
            ends = parts_of[(i, a)]
            for cols in [slice(c0, c1) for c0, c1 in zip((0,) + ends, ends)]:
                if n % 2 == 0:
                    nc.vector.tensor_copy(staged[:, cols], windows[(i, a)][:, cols])
                    nc.sync.dma_start(out[i, a * P : (a + 1) * P, cols], staged[:, cols])
                else:
                    nc.scalar.copy(staged[:, cols], windows[(i, a)][:, cols])
                    nc.scalar.dma_start(out[i, a * P : (a + 1) * P, cols], staged[:, cols])
